import numpy as np, ml_dtypes
CORES = [1,2,5,7,57,58,61,63,73,74,77,79]
N = 12
S, B = 3, 128
def setup_inputs(rng):
    a = (rng.standard_normal((128, 128), dtype=np.float32) / 8).astype(ml_dtypes.bfloat16)
    return {"x": (rng.standard_normal((N, 128, S * B), dtype=np.float32) / 2).astype(ml_dtypes.bfloat16), "a": np.broadcast_to(a, (N, 128, 128)).copy()}
def reference(x, a):
    X, A = x.astype(np.float64), a.astype(np.float64)
    y = np.zeros((N, 128, S * B)); h = np.zeros((128, B))
    for r in range(N):
        for s in range(S):
            h = np.tanh(A[r].T @ h + X[r][:, B * s:B * s + B])
            y[r][:, B * s:B * s + B] = h
    return {"y": y.astype(ml_dtypes.bfloat16)}

@@ -1,0 +1,190 @@
+from concourse.bass import DstId, RemoteDMATransfer
+from concourse.mybir import AluOpType, ActivationFunctionType
+
+N, S, B = 12, 3, 128
+K = 2
+W = B // K
+LOOK = 2
+NB = 8
+
+SCRATCH = {
+    "xl": ("sbuf", [128, S, K, W], "bfloat16"),
+    "xs": ("sbuf", [128, K, S, W], "bfloat16"),
+    "xw": ("sbuf", [128, N, S, W], "bfloat16"),
+    "al": ("sbuf", [128, 128], "bfloat16"),
+    "ones": ("sbuf", [128, 128], "bfloat16"),
+    "ident": ("sbuf", [128, 128], "bfloat16"),
+    "hs": ("sbuf", [128, N * S, W], "bfloat16"),
+    "h0": ("sbuf", [128, W], "bfloat16"),
+    "yl": ("sbuf", [128, K, S, W], "bfloat16"),
+    "yo": ("sbuf", [128, S, K, W], "bfloat16"),
+}
+for _b in range(NB):
+    SCRATCH["ps%d" % _b] = ("psum", [128, 512], "float32")
+SEMAPHORES = ["ldx", "lda", "fill", "idn", "rl", "mm", "hh", "ha", "ya", "yc", "st", "sent"] + ["xa%d" % r for r in range(N)]
+
+
+def _bits(mask):
+    return [b for b in range(32) if (mask >> b) & 1]
+
+
+def _split(bits, n):
+    per = 1
+    while per * 2 * n <= len(bits):
+        per *= 2
+    return [sum(1 << b for b in bits[i * per:(i + 1) * per]) for i in range(n)]
+
+
+def _count(mask):
+    return len(_bits(mask))
+
+
+def _plan(cores, topo):
+    groups = []
+    for r, c in enumerate(cores):
+        if groups and topo.chip(cores[groups[-1][0]]) == topo.chip(c):
+            groups[-1].append(r)
+        else:
+            groups.append([r])
+    dies = sorted(set(topo.die(c) for c in cores))
+    workers = [None] * len(groups)
+    for p in reversed(range(len(groups))):
+        later = [cores[w] for ws in workers[p + 1:] for w in ws]
+        workers[p] = [[r for r in groups[p] if topo.die(cores[r]) == d
+                       and all(topo.may_write(cores[r], c) for c in later)][-1] for d in dies]
+    first = [groups[0][0]] + [groups[1][0]] * (len(groups) - 1)
+    return groups, workers, first
+
+
+def _scatter(r, cores, topo, groups, workers, first):
+    src = cores[r]
+    tg = [(cores[workers[p][k]], k) for p in reversed(range(len(groups))) if first[p] <= r <= groups[p][-1]
+          for k in range(K) if workers[p][k] != r]
+    off = [t for t in tg if topo.chip(t[0]) != topo.chip(src)]
+    on = [t for t in tg if topo.chip(t[0]) == topo.chip(src)]
+    off_bits = _bits(topo.mask(src, off[0][0])) if off else []
+    on_bits = [b for b in _bits(topo.mask(src, on[0][0])) if b not in off_bits] if on else []
+    out = [(d, k, m) for (d, k), m in zip(off, _split(off_bits, max(1, len(off))))]
+    out += [(d, k, m) for (d, k), m in zip(on, _split(on_bits, max(1, len(on))))]
+    return out
+
+
+def _returns(p, k, cores, topo, groups, workers):
+    me = workers[p][k]
+    gr = groups[p]
+    batches = [gr[:len(gr) // 2], gr[len(gr) // 2:]] if p == len(groups) - 1 else [gr]
+    out = []
+    for bt in batches:
+        ds = [r for r in bt if r != me]
+        if ds:
+            out.append((S * bt[-1] + S - 1, list(zip(ds, _split(_bits(topo.mask(cores[me], cores[ds[0]])), len(ds))))))
+    return out
+
+
+def rank_program(g, core, T, topo):
+    rank = T.rank_of(core)
+    if rank is None:
+        return
+    cores = list(T.cores)
+    sem = T.sem
+    groups, workers, first = _plan(cores, topo)
+    P = len(groups)
+    p = [i for i in range(P) if rank in groups[i]][0]
+    worker = rank in workers[p]
+    k = workers[p].index(rank) if worker else None
+    sent = 0
+
+    def xfer(dst_core, mask, rsem, src, dst):
+        rid, pid, _ = topo.addr(dst_core)
+        return RemoteDMATransfer(dst_ids=[DstId(rid=rid, pnc=pid)], dma_engine_mask=mask, remote_sem=rsem, src=src, dst=dst)
+
+    g.sync.dma_start(T.xl[:, :, :, :], T.x[:, :]).then_inc(sem.ldx, 16)
+    if worker:
+        g.scalar.dma_start(T.al[:, :], T.a[:, :]).then_inc(sem.lda, 16)
+        g.vector.memset(T.ones[:, :], 1.0).then_inc(sem.fill, 1)
+        g.wait_ge(sem.fill, 1)
+        g.affine_select(T.ident[:, :], T.ones[:, :], [[-1, 128]], AluOpType.is_equal, 0.0, 0, 1).then_inc(sem.idn, 1)
+
+    sc = _scatter(rank, cores, topo, groups, workers, first)
+    ks = sorted(set(t[1] for t in sc))
+    g.vector.wait_ge(sem.ldx, 16)
+    for kk in ks:
+        g.vector.tensor_copy(T.xs[:, kk, :, :], T.xl[:, :, kk, :]).then_inc(sem.rl, 1)
+    g.wait_ge(sem.rl, len(ks))
+    g.remote_dma_fused([xfer(d, m, sem["xa%d" % rank], T.xs[:, kk, :, :], T.xw[:, rank, :, :]) for d, kk, m in sc],
+                       local_sem=sem.sent)
+    sent += sum(_count(m) for _, _, m in sc)
+
+    if worker:
+        t0, t1 = S * first[p], S * groups[p][-1] + S - 1
+        seen = {"tensor": set(), "scalar": set()}
+
+        def x_of(t, q, name):
+            r, s = t // S, t % S
+            if r not in seen[name]:
+                seen[name].add(r)
+                if r == rank:
+                    q.wait_ge(sem.ldx, 16)
+                else:
+                    m = [m for d, kk, m in _scatter(r, cores, topo, groups, workers, first) if d == core][0]
+                    q.wait_ge(sem["xa%d" % r], _count(m))
+            return T.xl[:, s, k, :] if r == rank else T.xw[:, r, s, :]
+
+        def bank(t):
+            return T["ps%d" % (t % NB)][:, 0:W]
+
+        def put_x(t):
+            g.tensor.matmul(bank(t), T.ident[:, :], x_of(t, g.tensor, "tensor"), True, False)
+
+        tm = t0 if p > 0 else t0 + 1
+        ha = _count(topo.mask(cores[workers[0][k]], core)) if p > 0 else 0
+        g.tensor.wait_ge(sem.idn, 1)
+        g.tensor.wait_ge(sem.lda, 16)
+        for t in range(tm, min(tm + LOOK, t1 + 1)):
+            put_x(t)
+        for t in range(tm, t1 + 1):
+            if t == t0:
+                g.tensor.wait_ge(sem.ha, ha)
+                prev = T.h0[:, :]
+            else:
+                g.tensor.wait_ge(sem.hh, t - t0)
+                prev = T.hs[:, t - 1, :]
+            g.tensor.matmul(bank(t), T.al[:, :], prev, False, True).then_inc(sem.mm, 1)
+            if t + LOOK <= t1:
+                put_x(t + LOOK)
+        for t in range(t0, t1 + 1):
+            if t < tm:
+                src = x_of(t, g.scalar, "scalar")
+            else:
+                g.scalar.wait_ge(sem.mm, t - tm + 1)
+                src = bank(t)
+            g.scalar.activation(T.hs[:, t, :], src, ActivationFunctionType.Tanh).then_inc(sem.hh, 1)
+
+        if p == 0:
+            g.wait_ge(sem.hh, t1 - t0 + 1)
+            for q in reversed(range(1, P)):
+                d = cores[workers[q][k]]
+                rid, pid, _ = topo.addr(d)
+                m = topo.mask(core, d)
+                g.remote_dma(T.h0[:, :], T.hs[:, t1, :], sem.ha, sem.sent, pid, rid, m)
+                sent += _count(m)
+        for tl, ds in _returns(p, k, cores, topo, groups, workers):
+            g.wait_ge(sem.hh, tl - t0 + 1)
+            g.remote_dma_fused([xfer(cores[r], m, sem.ya, T.hs[:, S * r:S * r + S, :], T.yl[:, k, :, :]) for r, m in ds],
+                               local_sem=sem.sent)
+            sent += sum(_count(m) for _, m in ds)
+        g.vector.wait_ge(sem.hh, S * rank + S - t0)
+        g.vector.tensor_copy(T.yo[:, :, k, :], T.hs[:, S * rank:S * rank + S, :]).then_inc(sem.yc, 1)
+
+    ya = 0
+    for kk in range(K):
+        if workers[p][kk] != rank:
+            ya += sum(_count(m) for _, ds in _returns(p, kk, cores, topo, groups, workers) for r, m in ds if r == rank)
+    g.vector.wait_ge(sem.ya, ya)
+    for kk in range(K):
+        if workers[p][kk] != rank:
+            g.vector.tensor_copy(T.yo[:, :, kk, :], T.yl[:, kk, :, :]).then_inc(sem.yc, 1)
+    g.sync.wait_ge(sem.yc, K)
+    g.sync.dma_start(T.y[:, :], T.yo[:, :, :, :]).then_inc(sem.st, 16)
+    g.sync.wait_ge(sem.st, 16)
+    g.wait_ge(sem.sent, sent)

@@ -4,24 +4,26 @@ from concourse.mybir import AluOpType, ActivationFunctionType
 N, S, B = 12, 3, 128
 K = 2
 W = B // K
-LOOK = 2
 NB = 8
 
 SCRATCH = {
     "xl": ("sbuf", [128, S, K, W], "bfloat16"),
     "xs": ("sbuf", [128, K, S, W], "bfloat16"),
     "xw": ("sbuf", [128, N, S, W], "bfloat16"),
+    "xf": ("sbuf", [128, N, S, K, W], "bfloat16"),
     "al": ("sbuf", [128, 128], "bfloat16"),
     "ones": ("sbuf", [128, 128], "bfloat16"),
     "ident": ("sbuf", [128, 128], "bfloat16"),
     "hs": ("sbuf", [128, N * S, W], "bfloat16"),
-    "h0": ("sbuf", [128, W], "bfloat16"),
+    "hf": ("sbuf", [128, N * S, K, W], "bfloat16"),
+    "h0": ("sbuf", [128, K, W], "bfloat16"),
     "yl": ("sbuf", [128, K, S, W], "bfloat16"),
     "yo": ("sbuf", [128, S, K, W], "bfloat16"),
 }
 for _b in range(NB):
     SCRATCH["ps%d" % _b] = ("psum", [128, 512], "float32")
-SEMAPHORES = ["ldx", "lda", "fill", "idn", "rl", "mm", "hh", "ha", "ya", "yc", "st", "sent"] + ["xa%d" % r for r in range(N)]
+SEMAPHORES = (["ldx", "lda", "fill", "idn", "rl", "ya", "yc", "st", "sent"] + ["xa%d" % r for r in range(N)]
+              + ["%s%d" % (n, j) for n in ("mm", "hh", "ha") for j in range(K)])
 
 
 def _bits(mask):
@@ -46,39 +48,52 @@ def _plan(cores, topo):
             groups[-1].append(r)
         else:
             groups.append([r])
+    later = [r for gr in groups[1:] for r in gr]
     dies = sorted(set(topo.die(c) for c in cores))
-    workers = [None] * len(groups)
-    for p in reversed(range(len(groups))):
-        later = [cores[w] for ws in workers[p + 1:] for w in ws]
-        workers[p] = [[r for r in groups[p] if topo.die(cores[r]) == d
-                       and all(topo.may_write(cores[r], c) for c in later)][-1] for d in dies]
-    first = [groups[0][0]] + [groups[1][0]] * (len(groups) - 1)
-    return groups, workers, first
+    workers = [[r for r in groups[0] if topo.die(cores[r]) == d
+                and all(topo.may_write(cores[r], cores[q]) for q in later)][-1] for d in dies]
+    return groups, workers
 
 
-def _scatter(r, cores, topo, groups, workers, first):
-    src = cores[r]
-    tg = [(cores[workers[p][k]], k) for p in reversed(range(len(groups))) if first[p] <= r <= groups[p][-1]
-          for k in range(K) if workers[p][k] != r]
-    off = [t for t in tg if topo.chip(t[0]) != topo.chip(src)]
-    on = [t for t in tg if topo.chip(t[0]) == topo.chip(src)]
-    off_bits = _bits(topo.mask(src, off[0][0])) if off else []
-    on_bits = [b for b in _bits(topo.mask(src, on[0][0])) if b not in off_bits] if on else []
-    out = [(d, k, m) for (d, k), m in zip(off, _split(off_bits, max(1, len(off))))]
-    out += [(d, k, m) for (d, k), m in zip(on, _split(on_bits, max(1, len(on))))]
+def _scatter(r, cores, topo, workers):
+    tg = [(cores[workers[k]], k) for k in range(K) if workers[k] != r]
+    return [(d, k, m) for (d, k), m in zip(tg, _split(_bits(topo.mask(cores[r], tg[0][0])), len(tg)))]
+
+
+def _returns(k, cores, topo, groups, workers):
+    ds = [r for r in groups[0] if r != workers[k]]
+    return list(zip(ds, _split(_bits(topo.mask(cores[workers[k]], cores[ds[0]])), len(ds))))
+
+
+def _xsend(r, cores, topo, groups):
+    p = [i for i in range(len(groups)) if r in groups[i]][0]
+    on = [q for q in groups[p] if q > r]
+    out, used = [], []
+    if p < len(groups) - 1:
+        partner = groups[-1][groups[p].index(r)]
+        used = _bits(topo.mask(cores[r], cores[partner]))
+        out.append(([partner], sum(1 << b for b in used)))
+    if on:
+        out.append((on, sum(1 << b for b in _bits(topo.mask(cores[r], cores[on[0]])) if b not in used)))
     return out
 
 
-def _returns(p, k, cores, topo, groups, workers):
-    me = workers[p][k]
-    gr = groups[p]
-    batches = [gr[:len(gr) // 2], gr[len(gr) // 2:]] if p == len(groups) - 1 else [gr]
+def _forward(q, cores, topo, groups):
     out = []
-    for bt in batches:
-        ds = [r for r in bt if r != me]
-        if ds:
-            out.append((S * bt[-1] + S - 1, list(zip(ds, _split(_bits(topo.mask(cores[me], cores[ds[0]])), len(ds))))))
+    for gr in groups[1:-1]:
+        ds = [d for d in groups[-1] if d != q]
+        out.append((gr[groups[-1].index(q)], ds, topo.mask(cores[q], cores[ds[0]])))
     return out
+
+
+def _xcount(r, me, cores, topo, groups):
+    for ds, m in _xsend(r, cores, topo, groups):
+        if me in ds:
+            return _count(m)
+    for q in groups[-1]:
+        for src, ds, m in _forward(q, cores, topo, groups):
+            if src == r and me in ds:
+                return _count(m)
 
 
 def rank_program(g, core, T, topo):
@@ -87,36 +102,107 @@ def rank_program(g, core, T, topo):
         return
     cores = list(T.cores)
     sem = T.sem
-    groups, workers, first = _plan(cores, topo)
-    P = len(groups)
-    p = [i for i in range(P) if rank in groups[i]][0]
-    worker = rank in workers[p]
-    k = workers[p].index(rank) if worker else None
+    groups, workers = _plan(cores, topo)
+    p = [i for i in range(len(groups)) if rank in groups[i]][0]
+    solo = p > 0
+    worker = rank in workers
+    k = workers.index(rank) if worker else None
+    maker = groups[0][0] if groups[0][0] not in workers else None
+    tc = S * groups[0][-1] + S - 1
+    Tanh = ActivationFunctionType.Tanh
     sent = 0
 
-    def xfer(dst_core, mask, rsem, src, dst):
-        rid, pid, _ = topo.addr(dst_core)
-        return RemoteDMATransfer(dst_ids=[DstId(rid=rid, pnc=pid)], dma_engine_mask=mask, remote_sem=rsem, src=src, dst=dst)
+    def xfer(dst_ranks, mask, rsem, src, dst):
+        ids = [DstId(rid=topo.addr(cores[r])[0], pnc=topo.addr(cores[r])[1]) for r in dst_ranks]
+        return RemoteDMATransfer(dst_ids=ids, dma_engine_mask=mask, remote_sem=rsem, srcs=[src], dsts=[dst] * len(ids))
 
     g.sync.dma_start(T.xl[:, :, :, :], T.x[:, :]).then_inc(sem.ldx, 16)
-    if worker:
+    if worker or solo:
         g.scalar.dma_start(T.al[:, :], T.a[:, :]).then_inc(sem.lda, 16)
+    idn = 1
+    if solo or rank == maker or (worker and maker is None):
         g.vector.memset(T.ones[:, :], 1.0).then_inc(sem.fill, 1)
         g.wait_ge(sem.fill, 1)
         g.affine_select(T.ident[:, :], T.ones[:, :], [[-1, 128]], AluOpType.is_equal, 0.0, 0, 1).then_inc(sem.idn, 1)
 
-    sc = _scatter(rank, cores, topo, groups, workers, first)
+    if solo:
+        calls = _xsend(rank, cores, topo, groups)
+        if calls:
+            g.wait_ge(sem.ldx, 16)
+            g.remote_dma_fused([xfer(ds, m, sem["xa%d" % rank], T.xl[:, :, :, :], T.xf[:, rank, :, :, :]) for ds, m in calls],
+                               local_sem=sem.sent)
+            sent += sum(_count(m) for _, m in calls)
+        if p == len(groups) - 1:
+            for src, ds, m in _forward(rank, cores, topo, groups):
+                g.wait_ge(sem["xa%d" % src], _xcount(src, rank, cores, topo, groups))
+                g.remote_dma_fused([xfer(ds, m, sem["xa%d" % src], T.xf[:, src, :, :, :], T.xf[:, src, :, :, :])],
+                                   local_sem=sem.sent)
+                sent += _count(m)
+
+        t0, t1 = tc + 1, S * rank + S - 1
+        look = NB // K - 1
+        seen = set()
+
+        def bank(t, j):
+            return T["ps%d" % ((K * t + j) % NB)][:, 0:W]
+
+        def put_x(t):
+            r, s = t // S, t % S
+            if r not in seen:
+                seen.add(r)
+                if r == rank:
+                    g.tensor.wait_ge(sem.ldx, 16)
+                else:
+                    g.tensor.wait_ge(sem["xa%d" % r], _xcount(r, rank, cores, topo, groups))
+            for j in range(K):
+                g.tensor.matmul(bank(t, j), T.ident[:, :], T.xl[:, s, j, :] if r == rank else T.xf[:, r, s, j, :], True, False)
+
+        g.tensor.wait_ge(sem.idn, 1)
+        g.tensor.wait_ge(sem.lda, 16)
+        for t in range(t0, min(t0 + look, t1 + 1)):
+            put_x(t)
+        for t in range(t0, t1 + 1):
+            for j in range(K):
+                if t == t0:
+                    g.tensor.wait_ge(sem["ha%d" % j], _count(topo.mask(cores[workers[j]], core)))
+                    prev = T.h0[:, j, :]
+                else:
+                    g.tensor.wait_ge(sem["hh%d" % j], t - t0)
+                    prev = T.hf[:, t - 1, j, :]
+                g.tensor.matmul(bank(t, j), T.al[:, :], prev, False, True).then_inc(sem["mm%d" % j], 1)
+            if t + look <= t1:
+                put_x(t + look)
+        for t in range(t0, t1 + 1):
+            for j in range(K):
+                g.scalar.wait_ge(sem["mm%d" % j], t - t0 + 1)
+                g.scalar.activation(T.hf[:, t, j, :], bank(t, j), Tanh).then_inc(sem["hh%d" % j], 1)
+        for j in range(K):
+            g.sync.wait_ge(sem["hh%d" % j], t1 - t0 + 1)
+        g.sync.dma_start(T.y[:, :], T.hf[:, S * rank:S * rank + S, :, :]).then_inc(sem.st, 16)
+        g.sync.wait_ge(sem.st, 16)
+        g.wait_ge(sem.sent, sent)
+        return
+
+    sc = _scatter(rank, cores, topo, workers)
+    if rank == maker:
+        g.wait_ge(sem.idn, 1)
+        g.remote_dma_fused([xfer([T.rank_of(d)], m, sem.idn, T.ident[:, :], T.ident[:, :]) for d, kk, m in sc],
+                           local_sem=sem.sent)
+        sent += sum(_count(m) for _, _, m in sc)
+    if worker and maker is not None:
+        idn = [_count(m) for d, kk, m in _scatter(maker, cores, topo, workers) if d == core][0]
+
     ks = sorted(set(t[1] for t in sc))
     g.vector.wait_ge(sem.ldx, 16)
     for kk in ks:
         g.vector.tensor_copy(T.xs[:, kk, :, :], T.xl[:, :, kk, :]).then_inc(sem.rl, 1)
     g.wait_ge(sem.rl, len(ks))
-    g.remote_dma_fused([xfer(d, m, sem["xa%d" % rank], T.xs[:, kk, :, :], T.xw[:, rank, :, :]) for d, kk, m in sc],
+    g.remote_dma_fused([xfer([T.rank_of(d)], m, sem["xa%d" % rank], T.xs[:, kk, :, :], T.xw[:, rank, :, :]) for d, kk, m in sc],
                        local_sem=sem.sent)
     sent += sum(_count(m) for _, _, m in sc)
 
     if worker:
-        t0, t1 = S * first[p], S * groups[p][-1] + S - 1
+        look = 2
         seen = {"tensor": set(), "scalar": set()}
 
         def x_of(t, q, name):
@@ -126,64 +212,49 @@ def rank_program(g, core, T, topo):
                 if r == rank:
                     q.wait_ge(sem.ldx, 16)
                 else:
-                    m = [m for d, kk, m in _scatter(r, cores, topo, groups, workers, first) if d == core][0]
-                    q.wait_ge(sem["xa%d" % r], _count(m))
+                    q.wait_ge(sem["xa%d" % r], [_count(m) for d, kk, m in _scatter(r, cores, topo, workers) if d == core][0])
             return T.xl[:, s, k, :] if r == rank else T.xw[:, r, s, :]
 
-        def bank(t):
+        def bank1(t):
             return T["ps%d" % (t % NB)][:, 0:W]
 
-        def put_x(t):
-            g.tensor.matmul(bank(t), T.ident[:, :], x_of(t, g.tensor, "tensor"), True, False)
+        def put_x1(t):
+            g.tensor.matmul(bank1(t), T.ident[:, :], x_of(t, g.tensor, "tensor"), True, False)
 
-        tm = t0 if p > 0 else t0 + 1
-        ha = _count(topo.mask(cores[workers[0][k]], core)) if p > 0 else 0
-        g.tensor.wait_ge(sem.idn, 1)
+        g.tensor.wait_ge(sem.idn, idn)
         g.tensor.wait_ge(sem.lda, 16)
-        for t in range(tm, min(tm + LOOK, t1 + 1)):
-            put_x(t)
-        for t in range(tm, t1 + 1):
-            if t == t0:
-                g.tensor.wait_ge(sem.ha, ha)
-                prev = T.h0[:, :]
-            else:
-                g.tensor.wait_ge(sem.hh, t - t0)
-                prev = T.hs[:, t - 1, :]
-            g.tensor.matmul(bank(t), T.al[:, :], prev, False, True).then_inc(sem.mm, 1)
-            if t + LOOK <= t1:
-                put_x(t + LOOK)
-        for t in range(t0, t1 + 1):
-            if t < tm:
+        for t in range(1, 1 + look):
+            put_x1(t)
+        for t in range(1, tc + 1):
+            g.tensor.wait_ge(sem.hh0, t)
+            g.tensor.matmul(bank1(t), T.al[:, :], T.hs[:, t - 1, :], False, True).then_inc(sem.mm0, 1)
+            if t + look <= tc:
+                put_x1(t + look)
+        for t in range(0, tc + 1):
+            if t == 0:
                 src = x_of(t, g.scalar, "scalar")
             else:
-                g.scalar.wait_ge(sem.mm, t - tm + 1)
-                src = bank(t)
-            g.scalar.activation(T.hs[:, t, :], src, ActivationFunctionType.Tanh).then_inc(sem.hh, 1)
+                g.scalar.wait_ge(sem.mm0, t)
+                src = bank1(t)
+            g.scalar.activation(T.hs[:, t, :], src, Tanh).then_inc(sem.hh0, 1)
 
-        if p == 0:
-            g.wait_ge(sem.hh, t1 - t0 + 1)
-            for q in reversed(range(1, P)):
-                d = cores[workers[q][k]]
-                rid, pid, _ = topo.addr(d)
-                m = topo.mask(core, d)
-                g.remote_dma(T.h0[:, :], T.hs[:, t1, :], sem.ha, sem.sent, pid, rid, m)
-                sent += _count(m)
-        for tl, ds in _returns(p, k, cores, topo, groups, workers):
-            g.wait_ge(sem.hh, tl - t0 + 1)
-            g.remote_dma_fused([xfer(cores[r], m, sem.ya, T.hs[:, S * r:S * r + S, :], T.yl[:, k, :, :]) for r, m in ds],
-                               local_sem=sem.sent)
-            sent += sum(_count(m) for _, m in ds)
-        g.vector.wait_ge(sem.hh, S * rank + S - t0)
+        g.wait_ge(sem.hh0, tc + 1)
+        for r in reversed(range(groups[0][-1] + 1, N)):
+            rid, pid, _ = topo.addr(cores[r])
+            m = topo.mask(core, cores[r])
+            g.remote_dma(T.h0[:, k, :], T.hs[:, tc, :], sem["ha%d" % k], sem.sent, pid, rid, m)
+            sent += _count(m)
+        rt = _returns(k, cores, topo, groups, workers)
+        g.remote_dma_fused([xfer([r], m, sem.ya, T.hs[:, S * r:S * r + S, :], T.yl[:, k, :, :]) for r, m in rt],
+                           local_sem=sem.sent)
+        sent += sum(_count(m) for _, m in rt)
+        g.vector.wait_ge(sem.hh0, S * rank + S)
         g.vector.tensor_copy(T.yo[:, :, k, :], T.hs[:, S * rank:S * rank + S, :]).then_inc(sem.yc, 1)
 
-    ya = 0
-    for kk in range(K):
-        if workers[p][kk] != rank:
-            ya += sum(_count(m) for _, ds in _returns(p, kk, cores, topo, groups, workers) for r, m in ds if r == rank)
-    g.vector.wait_ge(sem.ya, ya)
-    for kk in range(K):
-        if workers[p][kk] != rank:
-            g.vector.tensor_copy(T.yo[:, :, kk, :], T.yl[:, kk, :, :]).then_inc(sem.yc, 1)
+    others = [kk for kk in range(K) if workers[kk] != rank]
+    g.vector.wait_ge(sem.ya, sum(_count(m) for kk in others for r, m in _returns(kk, cores, topo, groups, workers) if r == rank))
+    for kk in others:
+        g.vector.tensor_copy(T.yo[:, :, kk, :], T.yl[:, kk, :, :]).then_inc(sem.yc, 1)
     g.sync.wait_ge(sem.yc, K)
     g.sync.dma_start(T.y[:, :], T.yo[:, :, :, :]).then_inc(sem.st, 16)
     g.sync.wait_ge(sem.st, 16)

@@ -4,11 +4,15 @@ from concourse.mybir import AluOpType, ActivationFunctionType
 N, S, B = 12, 3, 128
 K = 2
 W = B // K
+Q = 2
+V = W // Q
+NZ = 2
 NB = 8
 
 SCRATCH = {
     "xl": ("sbuf", [128, S, K, W], "bfloat16"),
     "xs": ("sbuf", [128, K, S, W], "bfloat16"),
+    "xr": ("sbuf", [128, 2, K, S, W], "bfloat16"),
     "xw": ("sbuf", [128, N, S, W], "bfloat16"),
     "xf": ("sbuf", [128, N, S, K, W], "bfloat16"),
     "al": ("sbuf", [128, 128], "bfloat16"),
@@ -22,7 +26,7 @@ SCRATCH = {
 }
 for _b in range(NB):
     SCRATCH["ps%d" % _b] = ("psum", [128, 512], "float32")
-SEMAPHORES = (["ldx", "lda", "fill", "idn", "rl", "ya", "yc", "st", "sent"] + ["xa%d" % r for r in range(N)]
+SEMAPHORES = (["ldx", "lda", "fill", "idn", "rl", "ya", "yc", "st", "sent", "rv0", "rv1"] + ["xa%d" % r for r in range(N)]
               + ["%s%d" % (n, j) for n in ("mm", "hh", "ha") for j in range(K)])
 
 
@@ -52,12 +56,27 @@ def _plan(cores, topo):
     dies = sorted(set(topo.die(c) for c in cores))
     workers = [[r for r in groups[0] if topo.die(cores[r]) == d
                 and all(topo.may_write(cores[r], cores[q]) for q in later)][-1] for d in dies]
-    return groups, workers
+    return groups, workers, later[:-NZ], later[-NZ:]
+
+
+def _group(r, groups):
+    return [gr for gr in groups if r in gr][0]
 
 
 def _scatter(r, cores, topo, workers):
-    tg = [(cores[workers[k]], k) for k in range(K) if workers[k] != r]
-    return [(d, k, m) for (d, k), m in zip(tg, _split(_bits(topo.mask(cores[r], tg[0][0])), len(tg)))]
+    tg = [(workers[k], k) for k in range(K) if workers[k] != r]
+    return [(w, k, m) for (w, k), m in zip(tg, _split(_bits(topo.mask(cores[r], cores[tg[0][0]])), len(tg)))]
+
+
+def _reaches(r, cores, topo, workers):
+    return all(topo.may_write(cores[r], cores[w]) for w in workers if w != r)
+
+
+def _via(r, cores, topo, groups, workers):
+    if _reaches(r, cores, topo, workers):
+        return r
+    cand = [q for q in _group(r, groups) if _reaches(q, cores, topo, workers)]
+    return ([q for q in cand if topo.die(cores[q]) == topo.die(cores[r])] or cand)[0]
 
 
 def _returns(k, cores, topo, groups, workers):
@@ -65,12 +84,12 @@ def _returns(k, cores, topo, groups, workers):
     return list(zip(ds, _split(_bits(topo.mask(cores[workers[k]], cores[ds[0]])), len(ds))))
 
 
-def _xsend(r, cores, topo, groups):
-    p = [i for i in range(len(groups)) if r in groups[i]][0]
-    on = [q for q in groups[p] if q > r]
+def _xsend(r, cores, topo, groups, solos):
+    gr = _group(r, groups)
+    on = [q for q in gr if q > r and q in solos]
     out, used = [], []
-    if p < len(groups) - 1:
-        partner = groups[-1][groups[p].index(r)]
+    if gr is not groups[-1] and [q for q in groups[-1] if q in solos]:
+        partner = groups[-1][gr.index(r)]
         used = _bits(topo.mask(cores[r], cores[partner]))
         out.append(([partner], sum(1 << b for b in used)))
     if on:
@@ -78,20 +97,21 @@ def _xsend(r, cores, topo, groups):
     return out
 
 
-def _forward(q, cores, topo, groups):
+def _forward(q, cores, topo, groups, solos):
     out = []
     for gr in groups[1:-1]:
-        ds = [d for d in groups[-1] if d != q]
-        out.append((gr[groups[-1].index(q)], ds, topo.mask(cores[q], cores[ds[0]])))
+        ds = [d for d in groups[-1] if d != q and d in solos]
+        if ds:
+            out.append((gr[groups[-1].index(q)], ds, topo.mask(cores[q], cores[ds[0]])))
     return out
 
 
-def _xcount(r, me, cores, topo, groups):
-    for ds, m in _xsend(r, cores, topo, groups):
+def _xcount(r, me, cores, topo, groups, solos):
+    for ds, m in _xsend(r, cores, topo, groups, solos):
         if me in ds:
             return _count(m)
     for q in groups[-1]:
-        for src, ds, m in _forward(q, cores, topo, groups):
+        for src, ds, m in _forward(q, cores, topo, groups, solos):
             if src == r and me in ds:
                 return _count(m)
 
@@ -102,9 +122,8 @@ def rank_program(g, core, T, topo):
         return
     cores = list(T.cores)
     sem = T.sem
-    groups, workers = _plan(cores, topo)
-    p = [i for i in range(len(groups)) if rank in groups[i]][0]
-    solo = p > 0
+    groups, workers, solos, tail = _plan(cores, topo)
+    solo = rank in solos
     worker = rank in workers
     k = workers.index(rank) if worker else None
     maker = groups[0][0] if groups[0][0] not in workers else None
@@ -114,7 +133,12 @@ def rank_program(g, core, T, topo):
 
     def xfer(dst_ranks, mask, rsem, src, dst):
         ids = [DstId(rid=topo.addr(cores[r])[0], pnc=topo.addr(cores[r])[1]) for r in dst_ranks]
-        return RemoteDMATransfer(dst_ids=ids, dma_engine_mask=mask, remote_sem=rsem, srcs=[src], dsts=[dst] * len(ids))
+        return (RemoteDMATransfer(dst_ids=ids, dma_engine_mask=mask, remote_sem=rsem, srcs=[src], dsts=[dst] * len(ids)),
+                _count(mask))
+
+    def fused(transfers):
+        g.remote_dma_fused([t for t, n in transfers], local_sem=sem.sent)
+        return sum(n for t, n in transfers)
 
     g.sync.dma_start(T.xl[:, :, :, :], T.x[:, :]).then_inc(sem.ldx, 16)
     if worker or solo:
@@ -124,21 +148,39 @@ def rank_program(g, core, T, topo):
         g.vector.memset(T.ones[:, :], 1.0).then_inc(sem.fill, 1)
         g.wait_ge(sem.fill, 1)
         g.affine_select(T.ident[:, :], T.ones[:, :], [[-1, 128]], AluOpType.is_equal, 0.0, 0, 1).then_inc(sem.idn, 1)
+    if rank == maker:
+        g.wait_ge(sem.idn, 1)
+        sent += fused([xfer([w], m, sem.idn, T.ident[:, :], T.ident[:, :]) for w, kk, m in _scatter(rank, cores, topo, workers)])
+    if worker and maker is not None:
+        idn = [_count(m) for w, kk, m in _scatter(maker, cores, topo, workers) if w == rank][0]
+
+    via = _via(rank, cores, topo, groups, workers)
+    ks = sorted(set(kk for w, kk, m in _scatter(rank, cores, topo, workers))) if via == rank else list(range(K))
+    g.vector.wait_ge(sem.ldx, 16)
+    for kk in ks:
+        g.vector.tensor_copy(T.xs[:, kk, :, :], T.xl[:, :, kk, :]).then_inc(sem.rl, 1)
+    g.wait_ge(sem.rl, len(ks))
+    if via == rank:
+        sent += fused([xfer([w], m, sem["xa%d" % rank], T.xs[:, kk, :, :], T.xw[:, rank, :, :])
+                       for w, kk, m in _scatter(rank, cores, topo, workers)])
+    else:
+        c = [r for r in _group(rank, groups) if r != via and _via(r, cores, topo, groups, workers) == via].index(rank)
+        sent += fused([xfer([via], topo.mask(core, cores[via]), sem["rv%d" % c], T.xs[:, :, :, :], T.xr[:, c, :, :, :])])
+
+    if rank not in groups[0]:
+        calls = _xsend(rank, cores, topo, groups, solos)
+        if calls:
+            sent += fused([xfer(ds, m, sem["xa%d" % rank], T.xl[:, :, :, :], T.xf[:, rank, :, :, :]) for ds, m in calls])
+        for c, r in enumerate([r for r in _group(rank, groups) if r != rank and _via(r, cores, topo, groups, workers) == rank]):
+            g.wait_ge(sem["rv%d" % c], _count(topo.mask(cores[r], core)))
+            sent += fused([xfer([w], m, sem["xa%d" % r], T.xr[:, c, kk, :, :], T.xw[:, r, :, :])
+                           for w, kk, m in _scatter(rank, cores, topo, workers)])
+        if rank in groups[-1]:
+            for src, ds, m in _forward(rank, cores, topo, groups, solos):
+                g.wait_ge(sem["xa%d" % src], _xcount(src, rank, cores, topo, groups, solos))
+                sent += fused([xfer(ds, m, sem["xa%d" % src], T.xf[:, src, :, :, :], T.xf[:, src, :, :, :])])
 
     if solo:
-        calls = _xsend(rank, cores, topo, groups)
-        if calls:
-            g.wait_ge(sem.ldx, 16)
-            g.remote_dma_fused([xfer(ds, m, sem["xa%d" % rank], T.xl[:, :, :, :], T.xf[:, rank, :, :, :]) for ds, m in calls],
-                               local_sem=sem.sent)
-            sent += sum(_count(m) for _, m in calls)
-        if p == len(groups) - 1:
-            for src, ds, m in _forward(rank, cores, topo, groups):
-                g.wait_ge(sem["xa%d" % src], _xcount(src, rank, cores, topo, groups))
-                g.remote_dma_fused([xfer(ds, m, sem["xa%d" % src], T.xf[:, src, :, :, :], T.xf[:, src, :, :, :])],
-                                   local_sem=sem.sent)
-                sent += _count(m)
-
         t0, t1 = tc + 1, S * rank + S - 1
         look = NB // K - 1
         seen = set()
@@ -153,7 +195,7 @@ def rank_program(g, core, T, topo):
                 if r == rank:
                     g.tensor.wait_ge(sem.ldx, 16)
                 else:
-                    g.tensor.wait_ge(sem["xa%d" % r], _xcount(r, rank, cores, topo, groups))
+                    g.tensor.wait_ge(sem["xa%d" % r], _xcount(r, rank, cores, topo, groups, solos))
             for j in range(K):
                 g.tensor.matmul(bank(t, j), T.ident[:, :], T.xl[:, s, j, :] if r == rank else T.xf[:, r, s, j, :], True, False)
 
@@ -179,83 +221,80 @@ def rank_program(g, core, T, topo):
         for j in range(K):
             g.sync.wait_ge(sem["hh%d" % j], t1 - t0 + 1)
         g.sync.dma_start(T.y[:, :], T.hf[:, S * rank:S * rank + S, :, :]).then_inc(sem.st, 16)
-        g.sync.wait_ge(sem.st, 16)
-        g.wait_ge(sem.sent, sent)
-        return
-
-    sc = _scatter(rank, cores, topo, workers)
-    if rank == maker:
-        g.wait_ge(sem.idn, 1)
-        g.remote_dma_fused([xfer([T.rank_of(d)], m, sem.idn, T.ident[:, :], T.ident[:, :]) for d, kk, m in sc],
-                           local_sem=sem.sent)
-        sent += sum(_count(m) for _, _, m in sc)
-    if worker and maker is not None:
-        idn = [_count(m) for d, kk, m in _scatter(maker, cores, topo, workers) if d == core][0]
-
-    ks = sorted(set(t[1] for t in sc))
-    g.vector.wait_ge(sem.ldx, 16)
-    for kk in ks:
-        g.vector.tensor_copy(T.xs[:, kk, :, :], T.xl[:, :, kk, :]).then_inc(sem.rl, 1)
-    g.wait_ge(sem.rl, len(ks))
-    g.remote_dma_fused([xfer([T.rank_of(d)], m, sem["xa%d" % rank], T.xs[:, kk, :, :], T.xw[:, rank, :, :]) for d, kk, m in sc],
-                       local_sem=sem.sent)
-    sent += sum(_count(m) for _, _, m in sc)
 
     if worker:
-        look = 2
+        te = N * S - 1
+        look = NB // Q - 1
         seen = {"tensor": set(), "scalar": set()}
 
-        def x_of(t, q, name):
+        def x_of(t, q, queue, name):
             r, s = t // S, t % S
             if r not in seen[name]:
                 seen[name].add(r)
                 if r == rank:
-                    q.wait_ge(sem.ldx, 16)
+                    queue.wait_ge(sem.ldx, 16)
                 else:
-                    q.wait_ge(sem["xa%d" % r], [_count(m) for d, kk, m in _scatter(r, cores, topo, workers) if d == core][0])
-            return T.xl[:, s, k, :] if r == rank else T.xw[:, r, s, :]
+                    bringer = _via(r, cores, topo, groups, workers)
+                    queue.wait_ge(sem["xa%d" % r], [_count(m) for w, kk, m in _scatter(bringer, cores, topo, workers) if w == rank][0])
+            return T.xl[:, s, k, V * q:V * q + V] if r == rank else T.xw[:, r, s, V * q:V * q + V]
 
-        def bank1(t):
-            return T["ps%d" % (t % NB)][:, 0:W]
+        def bankw(t, q):
+            return T["ps%d" % ((Q * t + q) % NB)][:, 0:V]
 
-        def put_x1(t):
-            g.tensor.matmul(bank1(t), T.ident[:, :], x_of(t, g.tensor, "tensor"), True, False)
+        def put_xw(t):
+            for q in range(Q):
+                g.tensor.matmul(bankw(t, q), T.ident[:, :], x_of(t, q, g.tensor, "tensor"), True, False)
+
+        def wait_h(queue, n):
+            for q in range(Q):
+                queue.wait_ge(sem["hh%d" % q], n)
 
         g.tensor.wait_ge(sem.idn, idn)
         g.tensor.wait_ge(sem.lda, 16)
         for t in range(1, 1 + look):
-            put_x1(t)
-        for t in range(1, tc + 1):
-            g.tensor.wait_ge(sem.hh0, t)
-            g.tensor.matmul(bank1(t), T.al[:, :], T.hs[:, t - 1, :], False, True).then_inc(sem.mm0, 1)
-            if t + look <= tc:
-                put_x1(t + look)
-        for t in range(0, tc + 1):
-            if t == 0:
-                src = x_of(t, g.scalar, "scalar")
-            else:
-                g.scalar.wait_ge(sem.mm0, t)
-                src = bank1(t)
-            g.scalar.activation(T.hs[:, t, :], src, Tanh).then_inc(sem.hh0, 1)
+            put_xw(t)
+        for t in range(1, te + 1):
+            for q in range(Q):
+                g.tensor.wait_ge(sem["hh%d" % q], t)
+                g.tensor.matmul(bankw(t, q), T.al[:, :], T.hs[:, t - 1, V * q:V * q + V], False, True).then_inc(sem["mm%d" % q], 1)
+            if t + look <= te:
+                put_xw(t + look)
+        for t in range(0, te + 1):
+            for q in range(Q):
+                if t == 0:
+                    src = x_of(t, q, g.scalar, "scalar")
+                else:
+                    g.scalar.wait_ge(sem["mm%d" % q], t)
+                    src = bankw(t, q)
+                g.scalar.activation(T.hs[:, t, V * q:V * q + V], src, Tanh).then_inc(sem["hh%d" % q], 1)
 
-        g.wait_ge(sem.hh0, tc + 1)
-        for r in reversed(range(groups[0][-1] + 1, N)):
+        wait_h(g, tc + 1)
+        for r in reversed(solos):
             rid, pid, _ = topo.addr(cores[r])
             m = topo.mask(core, cores[r])
             g.remote_dma(T.h0[:, k, :], T.hs[:, tc, :], sem["ha%d" % k], sem.sent, pid, rid, m)
             sent += _count(m)
-        rt = _returns(k, cores, topo, groups, workers)
-        g.remote_dma_fused([xfer([r], m, sem.ya, T.hs[:, S * r:S * r + S, :], T.yl[:, k, :, :]) for r, m in rt],
-                           local_sem=sem.sent)
-        sent += sum(_count(m) for _, m in rt)
-        g.vector.wait_ge(sem.hh0, S * rank + S)
+        sent += fused([xfer([r], m, sem.ya, T.hs[:, S * r:S * r + S, :], T.yl[:, k, :, :])
+                       for r, m in _returns(k, cores, topo, groups, workers)])
+        for r in tail:
+            rid, pid, _ = topo.addr(cores[r])
+            m = topo.mask(core, cores[r])
+            for s in range(S):
+                wait_h(g, S * r + s + 1)
+                g.remote_dma(T.yo[:, s, k, :], T.hs[:, S * r + s, :], sem.ya, sem.sent, pid, rid, m)
+                sent += _count(m)
+        wait_h(g.vector, S * rank + S)
         g.vector.tensor_copy(T.yo[:, :, k, :], T.hs[:, S * rank:S * rank + S, :]).then_inc(sem.yc, 1)
 
-    others = [kk for kk in range(K) if workers[kk] != rank]
-    g.vector.wait_ge(sem.ya, sum(_count(m) for kk in others for r, m in _returns(kk, cores, topo, groups, workers) if r == rank))
-    for kk in others:
-        g.vector.tensor_copy(T.yo[:, :, kk, :], T.yl[:, kk, :, :]).then_inc(sem.yc, 1)
-    g.sync.wait_ge(sem.yc, K)
-    g.sync.dma_start(T.y[:, :], T.yo[:, :, :, :]).then_inc(sem.st, 16)
+    if rank in groups[0]:
+        others = [kk for kk in range(K) if workers[kk] != rank]
+        g.vector.wait_ge(sem.ya, sum(_count(m) for kk in others for r, m in _returns(kk, cores, topo, groups, workers) if r == rank))
+        for kk in others:
+            g.vector.tensor_copy(T.yo[:, :, kk, :], T.yl[:, kk, :, :]).then_inc(sem.yc, 1)
+        g.sync.wait_ge(sem.yc, K)
+        g.sync.dma_start(T.y[:, :], T.yo[:, :, :, :]).then_inc(sem.st, 16)
+    if rank in tail:
+        g.sync.wait_ge(sem.ya, sum(S * _count(topo.mask(cores[w], core)) for w in workers))
+        g.sync.dma_start(T.y[:, :], T.yo[:, :, :, :]).then_inc(sem.st, 16)
     g.sync.wait_ge(sem.st, 16)
     g.wait_ge(sem.sent, sent)

from concourse.bass import DstId, RemoteDMATransfer
from concourse.mybir import AluOpType, ActivationFunctionType

N, S, B = 12, 3, 128
K = 2
W = B // K
Q = 2
V = W // Q
NZ = 2
NB = 8

SCRATCH = {
    "xl": ("sbuf", [128, S, K, W], "bfloat16"),
    "xs": ("sbuf", [128, K, S, W], "bfloat16"),
    "xr": ("sbuf", [128, 2, K, S, W], "bfloat16"),
    "xw": ("sbuf", [128, N, S, W], "bfloat16"),
    "xf": ("sbuf", [128, N, S, K, W], "bfloat16"),
    "al": ("sbuf", [128, 128], "bfloat16"),
    "ones": ("sbuf", [128, 128], "bfloat16"),
    "ident": ("sbuf", [128, 128], "bfloat16"),
    "hs": ("sbuf", [128, N * S, W], "bfloat16"),
    "hf": ("sbuf", [128, N * S, K, W], "bfloat16"),
    "h0": ("sbuf", [128, K, W], "bfloat16"),
    "yl": ("sbuf", [128, K, S, W], "bfloat16"),
    "yo": ("sbuf", [128, S, K, W], "bfloat16"),
}
for _b in range(NB):
    SCRATCH["ps%d" % _b] = ("psum", [128, 512], "float32")
SEMAPHORES = (["ldx", "lda", "fill", "idn", "rl", "ya", "yc", "st", "sent", "rv0", "rv1"] + ["xa%d" % r for r in range(N)]
              + ["%s%d" % (n, j) for n in ("mm", "hh", "ha") for j in range(K)])


def _bits(mask):
    return [b for b in range(32) if (mask >> b) & 1]


def _split(bits, n):
    per = 1
    while per * 2 * n <= len(bits):
        per *= 2
    return [sum(1 << b for b in bits[i * per:(i + 1) * per]) for i in range(n)]


def _count(mask):
    return len(_bits(mask))


def _plan(cores, topo):
    groups = []
    for r, c in enumerate(cores):
        if groups and topo.chip(cores[groups[-1][0]]) == topo.chip(c):
            groups[-1].append(r)
        else:
            groups.append([r])
    later = [r for gr in groups[1:] for r in gr]
    dies = sorted(set(topo.die(c) for c in cores))
    workers = [[r for r in groups[0] if topo.die(cores[r]) == d
                and all(topo.may_write(cores[r], cores[q]) for q in later)][-1] for d in dies]
    return groups, workers, later[:-NZ], later[-NZ:]


def _group(r, groups):
    return [gr for gr in groups if r in gr][0]


def _scatter(r, cores, topo, workers):
    tg = [(workers[k], k) for k in range(K) if workers[k] != r]
    return [(w, k, m) for (w, k), m in zip(tg, _split(_bits(topo.mask(cores[r], cores[tg[0][0]])), len(tg)))]


def _reaches(r, cores, topo, workers):
    return all(topo.may_write(cores[r], cores[w]) for w in workers if w != r)


def _via(r, cores, topo, groups, workers):
    if _reaches(r, cores, topo, workers):
        return r
    cand = [q for q in _group(r, groups) if _reaches(q, cores, topo, workers)]
    return ([q for q in cand if topo.die(cores[q]) == topo.die(cores[r])] or cand)[0]


def _returns(k, cores, topo, groups, workers):
    ds = [r for r in groups[0] if r != workers[k]]
    return list(zip(ds, _split(_bits(topo.mask(cores[workers[k]], cores[ds[0]])), len(ds))))


def _xsend(r, cores, topo, groups, solos):
    gr = _group(r, groups)
    on = [q for q in gr if q > r and q in solos]
    out, used = [], []
    if gr is not groups[-1] and [q for q in groups[-1] if q in solos]:
        partner = groups[-1][gr.index(r)]
        used = _bits(topo.mask(cores[r], cores[partner]))
        out.append(([partner], sum(1 << b for b in used)))
    if on:
        out.append((on, sum(1 << b for b in _bits(topo.mask(cores[r], cores[on[0]])) if b not in used)))
    return out


def _forward(q, cores, topo, groups, solos):
    out = []
    for gr in groups[1:-1]:
        ds = [d for d in groups[-1] if d != q and d in solos]
        if ds:
            out.append((gr[groups[-1].index(q)], ds, topo.mask(cores[q], cores[ds[0]])))
    return out


def _xcount(r, me, cores, topo, groups, solos):
    for ds, m in _xsend(r, cores, topo, groups, solos):
        if me in ds:
            return _count(m)
    for q in groups[-1]:
        for src, ds, m in _forward(q, cores, topo, groups, solos):
            if src == r and me in ds:
                return _count(m)


def rank_program(g, core, T, topo):
    rank = T.rank_of(core)
    if rank is None:
        return
    cores = list(T.cores)
    sem = T.sem
    groups, workers, solos, tail = _plan(cores, topo)
    solo = rank in solos
    worker = rank in workers
    k = workers.index(rank) if worker else None
    maker = groups[0][0] if groups[0][0] not in workers else None
    tc = S * groups[0][-1] + S - 1
    Tanh = ActivationFunctionType.Tanh
    sent = 0

    def xfer(dst_ranks, mask, rsem, src, dst):
        ids = [DstId(rid=topo.addr(cores[r])[0], pnc=topo.addr(cores[r])[1]) for r in dst_ranks]
        return (RemoteDMATransfer(dst_ids=ids, dma_engine_mask=mask, remote_sem=rsem, srcs=[src], dsts=[dst] * len(ids)),
                _count(mask))

    def fused(transfers):
        g.remote_dma_fused([t for t, n in transfers], local_sem=sem.sent)
        return sum(n for t, n in transfers)

    g.sync.dma_start(T.xl[:, :, :, :], T.x[:, :]).then_inc(sem.ldx, 16)
    if worker or solo:
        g.scalar.dma_start(T.al[:, :], T.a[:, :]).then_inc(sem.lda, 16)
    idn = 1
    if solo or rank == maker or (worker and maker is None):
        g.vector.memset(T.ones[:, :], 1.0).then_inc(sem.fill, 1)
        g.wait_ge(sem.fill, 1)
        g.affine_select(T.ident[:, :], T.ones[:, :], [[-1, 128]], AluOpType.is_equal, 0.0, 0, 1).then_inc(sem.idn, 1)
    if rank == maker:
        g.wait_ge(sem.idn, 1)
        sent += fused([xfer([w], m, sem.idn, T.ident[:, :], T.ident[:, :]) for w, kk, m in _scatter(rank, cores, topo, workers)])
    if worker and maker is not None:
        idn = [_count(m) for w, kk, m in _scatter(maker, cores, topo, workers) if w == rank][0]

    via = _via(rank, cores, topo, groups, workers)
    ks = sorted(set(kk for w, kk, m in _scatter(rank, cores, topo, workers))) if via == rank else list(range(K))
    g.vector.wait_ge(sem.ldx, 16)
    for kk in ks:
        g.vector.tensor_copy(T.xs[:, kk, :, :], T.xl[:, :, kk, :]).then_inc(sem.rl, 1)
    g.wait_ge(sem.rl, len(ks))
    if via == rank:
        sent += fused([xfer([w], m, sem["xa%d" % rank], T.xs[:, kk, :, :], T.xw[:, rank, :, :])
                       for w, kk, m in _scatter(rank, cores, topo, workers)])
    else:
        c = [r for r in _group(rank, groups) if r != via and _via(r, cores, topo, groups, workers) == via].index(rank)
        sent += fused([xfer([via], topo.mask(core, cores[via]), sem["rv%d" % c], T.xs[:, :, :, :], T.xr[:, c, :, :, :])])

    if rank not in groups[0]:
        calls = _xsend(rank, cores, topo, groups, solos)
        if calls:
            sent += fused([xfer(ds, m, sem["xa%d" % rank], T.xl[:, :, :, :], T.xf[:, rank, :, :, :]) for ds, m in calls])
        for c, r in enumerate([r for r in _group(rank, groups) if r != rank and _via(r, cores, topo, groups, workers) == rank]):
            g.wait_ge(sem["rv%d" % c], _count(topo.mask(cores[r], core)))
            sent += fused([xfer([w], m, sem["xa%d" % r], T.xr[:, c, kk, :, :], T.xw[:, r, :, :])
                           for w, kk, m in _scatter(rank, cores, topo, workers)])
        if rank in groups[-1]:
            for src, ds, m in _forward(rank, cores, topo, groups, solos):
                g.wait_ge(sem["xa%d" % src], _xcount(src, rank, cores, topo, groups, solos))
                sent += fused([xfer(ds, m, sem["xa%d" % src], T.xf[:, src, :, :, :], T.xf[:, src, :, :, :])])

    if solo:
        t0, t1 = tc + 1, S * rank + S - 1
        look = NB // K - 1
        seen = set()

        def bank(t, j):
            return T["ps%d" % ((K * t + j) % NB)][:, 0:W]

        def put_x(t):
            r, s = t // S, t % S
            if r not in seen:
                seen.add(r)
                if r == rank:
                    g.tensor.wait_ge(sem.ldx, 16)
                else:
                    g.tensor.wait_ge(sem["xa%d" % r], _xcount(r, rank, cores, topo, groups, solos))
            for j in range(K):
                g.tensor.matmul(bank(t, j), T.ident[:, :], T.xl[:, s, j, :] if r == rank else T.xf[:, r, s, j, :], True, False)

        g.tensor.wait_ge(sem.idn, 1)
        g.tensor.wait_ge(sem.lda, 16)
        for t in range(t0, min(t0 + look, t1 + 1)):
            put_x(t)
        for t in range(t0, t1 + 1):
            for j in range(K):
                if t == t0:
                    g.tensor.wait_ge(sem["ha%d" % j], _count(topo.mask(cores[workers[j]], core)))
                    prev = T.h0[:, j, :]
                else:
                    g.tensor.wait_ge(sem["hh%d" % j], t - t0)
                    prev = T.hf[:, t - 1, j, :]
                g.tensor.matmul(bank(t, j), T.al[:, :], prev, False, True).then_inc(sem["mm%d" % j], 1)
            if t + look <= t1:
                put_x(t + look)
        for t in range(t0, t1 + 1):
            for j in range(K):
                g.scalar.wait_ge(sem["mm%d" % j], t - t0 + 1)
                g.scalar.activation(T.hf[:, t, j, :], bank(t, j), Tanh).then_inc(sem["hh%d" % j], 1)
        for j in range(K):
            g.sync.wait_ge(sem["hh%d" % j], t1 - t0 + 1)
        g.sync.dma_start(T.y[:, :], T.hf[:, S * rank:S * rank + S, :, :]).then_inc(sem.st, 16)

    if worker:
        te = N * S - 1
        look = NB // Q - 1
        seen = {"tensor": set(), "scalar": set()}

        def x_of(t, q, queue, name):
            r, s = t // S, t % S
            if r not in seen[name]:
                seen[name].add(r)
                if r == rank:
                    queue.wait_ge(sem.ldx, 16)
                else:
                    bringer = _via(r, cores, topo, groups, workers)
                    queue.wait_ge(sem["xa%d" % r], [_count(m) for w, kk, m in _scatter(bringer, cores, topo, workers) if w == rank][0])
            return T.xl[:, s, k, V * q:V * q + V] if r == rank else T.xw[:, r, s, V * q:V * q + V]

        def bankw(t, q):
            return T["ps%d" % ((Q * t + q) % NB)][:, 0:V]

        def put_xw(t):
            for q in range(Q):
                g.tensor.matmul(bankw(t, q), T.ident[:, :], x_of(t, q, g.tensor, "tensor"), True, False)

        def wait_h(queue, n):
            for q in range(Q):
                queue.wait_ge(sem["hh%d" % q], n)

        g.tensor.wait_ge(sem.idn, idn)
        g.tensor.wait_ge(sem.lda, 16)
        for t in range(1, 1 + look):
            put_xw(t)
        for t in range(1, te + 1):
            for q in range(Q):
                g.tensor.wait_ge(sem["hh%d" % q], t)
                g.tensor.matmul(bankw(t, q), T.al[:, :], T.hs[:, t - 1, V * q:V * q + V], False, True).then_inc(sem["mm%d" % q], 1)
            if t + look <= te:
                put_xw(t + look)
        for t in range(0, te + 1):
            for q in range(Q):
                if t == 0:
                    src = x_of(t, q, g.scalar, "scalar")
                else:
                    g.scalar.wait_ge(sem["mm%d" % q], t)
                    src = bankw(t, q)
                g.scalar.activation(T.hs[:, t, V * q:V * q + V], src, Tanh).then_inc(sem["hh%d" % q], 1)

        wait_h(g, tc + 1)
        for r in reversed(solos):
            rid, pid, _ = topo.addr(cores[r])
            m = topo.mask(core, cores[r])
            g.remote_dma(T.h0[:, k, :], T.hs[:, tc, :], sem["ha%d" % k], sem.sent, pid, rid, m)
            sent += _count(m)
        sent += fused([xfer([r], m, sem.ya, T.hs[:, S * r:S * r + S, :], T.yl[:, k, :, :])
                       for r, m in _returns(k, cores, topo, groups, workers)])
        for r in tail:
            rid, pid, _ = topo.addr(cores[r])
            m = topo.mask(core, cores[r])
            for s in range(S):
                wait_h(g, S * r + s + 1)
                g.remote_dma(T.yo[:, s, k, :], T.hs[:, S * r + s, :], sem.ya, sem.sent, pid, rid, m)
                sent += _count(m)
        wait_h(g.vector, S * rank + S)
        g.vector.tensor_copy(T.yo[:, :, k, :], T.hs[:, S * rank:S * rank + S, :]).then_inc(sem.yc, 1)

    if rank in groups[0]:
        others = [kk for kk in range(K) if workers[kk] != rank]
        g.vector.wait_ge(sem.ya, sum(_count(m) for kk in others for r, m in _returns(kk, cores, topo, groups, workers) if r == rank))
        for kk in others:
            g.vector.tensor_copy(T.yo[:, :, kk, :], T.yl[:, kk, :, :]).then_inc(sem.yc, 1)
        g.sync.wait_ge(sem.yc, K)
        g.sync.dma_start(T.y[:, :], T.yo[:, :, :, :]).then_inc(sem.st, 16)
    if rank in tail:
        g.sync.wait_ge(sem.ya, sum(S * _count(topo.mask(cores[w], core)) for w in workers))
        g.sync.dma_start(T.y[:, :], T.yo[:, :, :, :]).then_inc(sem.st, 16)
    g.sync.wait_ge(sem.st, 16)
    g.wait_ge(sem.sent, sent)
